import numpy as np
import ml_dtypes


def mxq(x, axis, fmt="e4m3"):
    dtype, down = {"e4m3": (ml_dtypes.float8_e4m3fn, 7), "e5m2": (ml_dtypes.float8_e5m2, 14)}[fmt]
    v = np.moveaxis(np.asarray(x, np.float32).astype(ml_dtypes.bfloat16).astype(np.float64), axis, -1)
    blocks = v.reshape(v.shape[:-1] + (-1, 32))
    amax = np.abs(blocks).max(-1, keepdims=True)
    byte = np.maximum(np.where(amax > 0, np.frexp(amax)[1] - 1 + 127, 0) - down, 1)
    scale = np.exp2(byte - 127.0)
    codes = (blocks / scale).astype(np.float32).astype(dtype).astype(np.float64)
    return np.moveaxis((codes * scale).reshape(v.shape), -1, axis)


WIDE = False


def mx_kscale(k):
    if not WIDE:
        return np.ones(k)
    levels = np.array([10, -10, 5, -5, 0])
    if k % 512:
        return np.exp2(np.random.permutation(np.resize(levels, k // 32))).repeat(32)
    a = np.empty((k // 512, 16))
    for p in range(k // 512):
        a[p, :8] = np.random.permutation(np.resize(levels, 8))
        for g in range(8):
            far = levels[np.abs(levels - a[p, g]) >= 10]
            a[p, g + 8] = far[np.random.randint(len(far))]
    return np.exp2(a.ravel()).repeat(32)


def f64(x):
    return np.asarray(x).astype(np.float64)


def striped(idx):
    return np.tile(idx.reshape(-1, 16).T, (8, 1)).astype(np.uint16)


def unstriped(offs):
    return offs[:16].T.reshape(-1).astype(np.int64)


def pack_weight(w):
    k, n = w.shape
    w = f64(np.asarray(w, np.float32).astype(ml_dtypes.bfloat16)).reshape(k // 32, 32, n)
    amax = np.abs(w).max(1)
    byte = np.clip(np.where(amax > 0, np.frexp(amax)[1] - 1 + 127 - 7, 1), 1, 254)
    scaled = (w * np.exp2(127.0 - byte)[:, None, :]).reshape(k, n).astype(np.float32)
    words = np.ascontiguousarray(scaled.reshape(k // 512, 128, 4, n).transpose(0, 1, 3, 2)).astype(ml_dtypes.float8_e4m3fn).view(np.uint8)
    return words, np.ascontiguousarray(byte.astype(np.uint8).reshape(k // 512, 16, n))


def unpack_weight(words, scales):
    g, p, n, _ = words.shape
    vals = np.ascontiguousarray(words).view(ml_dtypes.float8_e4m3fn).astype(np.float64) * np.repeat(np.exp2(scales.astype(np.float64) - 127.0), 8, axis=1)[..., None]
    return vals.transpose(0, 1, 3, 2).reshape(g * 512, n)


K, T, S, V = 1024, 2048, 512, 512


def setup_inputs():
    n = np.random.standard_normal
    s = mx_kscale(K)[:, None]
    packed_xT = pack_weight(n((K, T)) * s)
    return {
        "x_words": packed_xT[0],
        "x_scales": packed_xT[1],
        "hT": (n((K, V)) / np.sqrt(K) / s).astype(np.float32),
        "goal": ((np.random.uniform(size=(V, S)) < 0.004) * 0.9).astype(np.float32),
        "wgt": (np.random.uniform(20.0, 60.0, (V, 1))).astype(np.float32),
        "offs": striped(np.random.permutation(T)[:S]),
    }


def reference(x_words, x_scales, hT, goal, wgt, offs):
    hTq = mxq(f64(hT), 0, "e4m3")
    xq = unpack_weight(x_words, x_scales)[:, unstriped(offs)]
    y = hTq.T @ xq
    ee = np.exp(y)
    total = ee.sum(axis=1, keepdims=True)
    p = ee / total
    lse = np.log(total)
    gg = p + p * (0.2 * lse)
    return f64(wgt) * (gg - f64(goal) - 0.0002)

@@ -1,0 +1,183 @@
+import math
+from contextlib import ExitStack
+
+import concourse.mybir as mybir
+
+K, T, S, V = 1024, 2048, 512, 512
+FLOPS = 2 * K * S * V
+
+F32 = mybir.dt.float32
+BF16 = mybir.dt.bfloat16
+I32 = mybir.dt.int32
+U32 = mybir.dt.uint32
+U16 = mybir.dt.uint16
+U8 = mybir.dt.uint8
+FP8X4 = mybir.dt.float8_e4m3fn_x4
+ALU = mybir.AluOpType
+ACT = mybir.ActivationFunctionType
+
+P = 128
+PACK = 4
+K_PASS = P * PACK
+PASSES = K // K_PASS
+TILES = V // P
+HALF = V // 2
+
+Z_COEF = 0.2
+SMOOTH = 0.0002
+
+NODES = 80
+STEP = 0.42
+FIRST = -29.8
+LOG_CONST = STEP * sum(math.exp(-math.exp(FIRST + STEP * n)) for n in range(NODES))
+
+
+def tile_picked_yzloss_grad_p_kernel(tc, x_words, x_scales, hT, goal, wgt, offs, out):
+    nc = tc.nc
+    with ExitStack() as ctx:
+        keep = ctx.enter_context(tc.tile_pool(name="keep", bufs=1))
+        psum = ctx.enter_context(tc.psum_pool(name="psum", bufs=1))
+
+        offsets = keep.tile([P, S // 16], U16, name="offsets")
+        words = [keep.tile([P, T], U32, name="words%d" % g, align_bytes=64) for g in range(PASSES)]
+        planes = keep.tile([P, T], U8, name="planes", align_bytes=64)
+        picked_words = [keep.tile([P, S], U32, name="picked_words%d" % g, align_bytes=64) for g in range(PASSES)]
+        picked_planes = keep.tile([P, S], U8, name="picked_planes", align_bytes=64)
+        h_raw = {(g, u): keep.tile([P, PACK, HALF], F32, name="h_raw%d%d" % (g, u), align_bytes=64)
+                 for g in range(PASSES) for u in range(2)}
+        goal_sb = [keep.tile([P, S], F32, name="goal%d" % i, align_bytes=64) for i in range(TILES)]
+        wgt_sb = keep.tile([P, TILES], F32, name="wgt_sb")
+        logits = [psum.tile([P, S], F32, name="logits%d" % i) for i in range(TILES)]
+
+        def load_words(g):
+            nc.sync.dma_start(out=words[g][:].bitcast(I32), in_=x_words[g].rearrange("p n t -> p (n t)").bitcast(I32))
+
+        def load_h(g, u):
+            rows = hT[g * K_PASS:(g + 1) * K_PASS, u * HALF:(u + 1) * HALF]
+            nc.sync.dma_start(out=h_raw[g, u][:], in_=rows.rearrange("(p j) w -> p j w", j=PACK))
+
+        def load_planes():
+            for q in range(4):
+                nc.sync.dma_start(out=planes[32 * q:32 * q + 4 * PASSES, :].bitcast(I32),
+                                  in_=x_scales[:, 4 * q:4 * q + 4, :].bitcast(I32))
+
+        def load_goal(i):
+            nc.sync.dma_start(out=goal_sb[i][:], in_=goal[i * P:(i + 1) * P, :])
+
+        nc.vector.memset(planes[:, :T // 2].bitcast(I32), 0)
+        nc.gpsimd.memset(planes[:, T // 2:].bitcast(I32), 0)
+        nc.sync.dma_start(offsets[:], offs)
+        load_words(0)
+        load_planes()
+        load_h(0, 0)
+        load_words(1)
+        load_h(1, 0)
+        load_h(0, 1)
+        load_h(1, 1)
+        with nc.allow_non_contiguous_dma(reason="one weight a partition"):
+            nc.gpsimd.dma_start(out=wgt_sb[:], in_=wgt.rearrange("(i p) o -> p (i o)", p=P))
+        for i in range(TILES):
+            load_goal(i)
+
+        index = keep.tile([P, NODES], F32, name="index")
+        nc.gpsimd.iota(index[:], [[1, NODES]], base=0, channel_multiplier=0, allow_small_or_imprecise_dtypes=True)
+        rates = keep.tile([P, NODES], F32, name="rates")
+        nc.scalar.activation(out=rates[:], in_=index[:], func=ACT.Exp, scale=STEP, bias=FIRST)
+        neg_rates = keep.tile([P, NODES], F32, name="neg_rates")
+        nc.vector.tensor_scalar(out=neg_rates[:], in0=rates[:], scalar1=-1.0, scalar2=None, op0=ALU.mult)
+        wgt_smooth = keep.tile([P, TILES], F32, name="wgt_smooth")
+        wgt_step = keep.tile([P, TILES], F32, name="wgt_step")
+        nc.vector.tensor_scalar(out=wgt_smooth[:], in0=wgt_sb[:], scalar1=SMOOTH, scalar2=None, op0=ALU.mult)
+        nc.vector.tensor_scalar(out=wgt_step[:], in0=wgt_sb[:], scalar1=-Z_COEF * STEP, scalar2=None, op0=ALU.mult)
+
+        h_bf, h_codes, h_scales = {}, {}, {}
+        stats = {}
+
+        def gather_words(g):
+            nc.vector.tensor_copy(out=picked_words[g][:], in_=words[g][:].indirect(offsets[:]))
+
+        def gather_planes():
+            nc.vector.tensor_copy(out=picked_planes[:], in_=planes[:].indirect(offsets[:]))
+
+        def cast(g, i, copy):
+            h_bf[g, i] = keep.tile([P, P, PACK], BF16, name="h_bf%d%d" % (g, i), align_bytes=64)
+            cols = slice((i % 2) * P, (i % 2 + 1) * P)
+            copy(out=h_bf[g, i][:].rearrange("p (c e) j -> p c j e", e=4),
+                 in_=h_raw[g, i // 2][:, :, cols].rearrange("p j (c e) -> p c j e", e=4))
+
+        def quantize(g, i):
+            h_codes[g, i] = keep.tile([P, P], U32, name="h_codes%d%d" % (g, i), align_bytes=64)
+            h_scales[g, i] = keep.tile([P, P], U8, name="h_scales%d%d" % (g, i), align_bytes=64)
+            nc.vector.quantize_mx(out=h_codes[g, i][:].bitcast(FP8X4), scales=h_scales[g, i][:],
+                                  in_=h_bf[g, i][:].rearrange("p c j -> p (c j)"))
+
+        def multiply(g, i):
+            nc.tensor.matmul_mx(out=logits[i][:], lhsT=h_codes[g, i][:].bitcast(FP8X4), lhsT_scale=h_scales[g, i][:],
+                                rhs=picked_words[g][:].bitcast(FP8X4), rhs_scale=picked_planes[4 * g:, :],
+                                start=(g == 0), stop=(g == PASSES - 1))
+
+        def stat(name, i):
+            stats[name, i] = keep.tile([P, 1], F32, name="%s%d" % (name, i))
+            return stats[name, i][:]
+
+        def row_max(i):
+            nc.vector.tensor_reduce(out=stat("neg_max", i), in_=logits[i][:], axis=mybir.AxisListType.X, op=ALU.max, negate=True)
+
+        expd = [keep.tile([P, S], F32, name="expd%d" % i, align_bytes=64) for i in range(TILES)]
+        target = [keep.tile([P, S], F32, name="target%d" % i, align_bytes=64) for i in range(TILES)]
+        result = [keep.tile([P, S], F32, name="result%d" % i, align_bytes=64) for i in range(TILES)]
+        decays = [keep.tile([P, NODES], F32, name="decays%d" % i) for i in range(TILES)]
+
+        def exponentiate(i):
+            nc.scalar.activation(out=expd[i][:], in_=logits[i][:], func=ACT.Exp, bias=stats["neg_max", i][:], scale=1.0,
+                                 accum_out=stat("total", i))
+            nc.scalar.activation(out=decays[i][:], in_=neg_rates[:], func=ACT.Exp, scale=stats["total", i][:],
+                                 accum_out=stat("decay_sum", i))
+
+        def shift(i):
+            nc.vector.tensor_scalar(out=stat("shift", i), in0=stats["neg_max", i][:], scalar1=1.0 / STEP,
+                                    scalar2=-(1.0 + Z_COEF * LOG_CONST) / (Z_COEF * STEP), op0=ALU.mult, op1=ALU.add)
+
+        def factor(i):
+            nc.vector.reciprocal(out=stat("inv_total", i), in_=stats["total", i][:])
+            nc.vector.tensor_scalar(out=stat("gain", i), in0=stats["inv_total", i][:], scalar1=wgt_step[:, i:i + 1],
+                                    scalar2=None, op0=ALU.mult)
+            nc.vector.tensor_scalar(out=stat("factor", i), in0=stats["decay_sum", i][:], scalar1=stats["shift", i][:],
+                                    scalar2=stats["gain", i][:], op0=ALU.add, op1=ALU.mult)
+
+        def weigh_goal(i, eng):
+            if eng == "s":
+                nc.scalar.activation(out=target[i][:], in_=goal_sb[i][:], func=ACT.Identity,
+                                     scale=wgt_sb[:, i:i + 1], bias=wgt_smooth[:, i:i + 1])
+            else:
+                (nc.vector if eng == "v" else nc.gpsimd).tensor_scalar(
+                    out=target[i][:], in0=goal_sb[i][:], scalar1=wgt_sb[:, i:i + 1],
+                    scalar2=wgt_smooth[:, i:i + 1], op0=ALU.mult, op1=ALU.add)
+
+        def finish(i):
+            nc.vector.scalar_tensor_tensor(out=result[i][:], in0=expd[i][:], scalar=stats["factor", i][:],
+                                           in1=target[i][:], op0=ALU.mult, op1=ALU.subtract)
+            nc.sync.dma_start(out=out[i * P:(i + 1) * P, :], in_=result[i][:])
+
+        on_v, on_s = nc.vector.tensor_copy, nc.scalar.copy
+        gather_planes()
+        for g in range(PASSES):
+            gather_words(g)
+        for u in range(2):
+            for g in range(PASSES):
+                for i in (2 * u, 2 * u + 1):
+                    cast(g, i, on_s if (i % 2 == 1 or (g, u) == (0, 0)) else on_v)
+                for i in (2 * u, 2 * u + 1):
+                    quantize(g, i)
+                    multiply(g, i)
+        for i in range(TILES):
+            weigh_goal(i, "g")
+        for i in range(TILES):
+            row_max(i)
+            exponentiate(i)
+            shift(i)
+            if i > 0:
+                factor(i - 1)
+        factor(TILES - 1)
+        for i in range(TILES):
+            finish(i)

@@ -1,4 +1,3 @@
-import math
 from contextlib import ExitStack
 
 import concourse.mybir as mybir
@@ -21,15 +20,14 @@ PACK = 4
 K_PASS = P * PACK
 PASSES = K // K_PASS
 TILES = V // P
-HALF = V // 2
 
 Z_COEF = 0.2
 SMOOTH = 0.0002
 
-NODES = 80
-STEP = 0.42
-FIRST = -29.8
-LOG_CONST = STEP * sum(math.exp(-math.exp(FIRST + STEP * n)) for n in range(NODES))
+NODES = 84
+STEP = 0.4
+FIRST = -30.0
+EULER = 0.5772156649015329
 
 
 def tile_picked_yzloss_grad_p_kernel(tc, x_words, x_scales, hT, goal, wgt, offs, out):
@@ -43,8 +41,8 @@ def tile_picked_yzloss_grad_p_kernel(tc, x_words, x_scales, hT, goal, wgt, offs,
         planes = keep.tile([P, T], U8, name="planes", align_bytes=64)
         picked_words = [keep.tile([P, S], U32, name="picked_words%d" % g, align_bytes=64) for g in range(PASSES)]
         picked_planes = keep.tile([P, S], U8, name="picked_planes", align_bytes=64)
-        h_raw = {(g, u): keep.tile([P, PACK, HALF], F32, name="h_raw%d%d" % (g, u), align_bytes=64)
-                 for g in range(PASSES) for u in range(2)}
+        h_raw = {(g, u): keep.tile([P, PACK, P], F32, name="h_raw%d%d" % (g, u), align_bytes=64)
+                 for g in range(PASSES) for u in range(TILES)}
         goal_sb = [keep.tile([P, S], F32, name="goal%d" % i, align_bytes=64) for i in range(TILES)]
         wgt_sb = keep.tile([P, TILES], F32, name="wgt_sb")
         logits = [psum.tile([P, S], F32, name="logits%d" % i) for i in range(TILES)]
@@ -53,7 +51,7 @@ def tile_picked_yzloss_grad_p_kernel(tc, x_words, x_scales, hT, goal, wgt, offs,
             nc.sync.dma_start(out=words[g][:].bitcast(I32), in_=x_words[g].rearrange("p n t -> p (n t)").bitcast(I32))
 
         def load_h(g, u):
-            rows = hT[g * K_PASS:(g + 1) * K_PASS, u * HALF:(u + 1) * HALF]
+            rows = hT[g * K_PASS:(g + 1) * K_PASS, u * P:(u + 1) * P]
             nc.sync.dma_start(out=h_raw[g, u][:], in_=rows.rearrange("(p j) w -> p j w", j=PACK))
 
         def load_planes():
@@ -69,13 +67,12 @@ def tile_picked_yzloss_grad_p_kernel(tc, x_words, x_scales, hT, goal, wgt, offs,
         nc.sync.dma_start(offsets[:], offs)
         load_words(0)
         load_planes()
-        load_h(0, 0)
         load_words(1)
-        load_h(1, 0)
-        load_h(0, 1)
-        load_h(1, 1)
+        for i in range(TILES):
+            for g in range(PASSES):
+                load_h(g, i)
         with nc.allow_non_contiguous_dma(reason="one weight a partition"):
-            nc.gpsimd.dma_start(out=wgt_sb[:], in_=wgt.rearrange("(i p) o -> p (i o)", p=P))
+            nc.sync.dma_start(out=wgt_sb[:], in_=wgt.rearrange("(i p) o -> p (i o)", p=P))
         for i in range(TILES):
             load_goal(i)
 
@@ -85,10 +82,15 @@ def tile_picked_yzloss_grad_p_kernel(tc, x_words, x_scales, hT, goal, wgt, offs,
         nc.scalar.activation(out=rates[:], in_=index[:], func=ACT.Exp, scale=STEP, bias=FIRST)
         neg_rates = keep.tile([P, NODES], F32, name="neg_rates")
         nc.vector.tensor_scalar(out=neg_rates[:], in0=rates[:], scalar1=-1.0, scalar2=None, op0=ALU.mult)
+        per_max = keep.tile([P, NODES], F32, name="per_max")
+        nc.vector.tensor_scalar(out=per_max[:], in0=rates[:], scalar1=-Z_COEF * STEP, scalar2=None, op0=ALU.mult)
+        log_term = keep.tile([P, NODES], F32, name="log_term")
+        nc.vector.tensor_scalar(out=log_term[:], in0=index[:], scalar1=-Z_COEF * STEP * STEP,
+                                scalar2=STEP * (1.0 - Z_COEF * (EULER + FIRST)), op0=ALU.mult, op1=ALU.add)
+        base = keep.tile([P, NODES], F32, name="base")
+        nc.vector.tensor_tensor(out=base[:], in0=log_term[:], in1=rates[:], op=ALU.mult)
         wgt_smooth = keep.tile([P, TILES], F32, name="wgt_smooth")
-        wgt_step = keep.tile([P, TILES], F32, name="wgt_step")
-        nc.vector.tensor_scalar(out=wgt_smooth[:], in0=wgt_sb[:], scalar1=SMOOTH, scalar2=None, op0=ALU.mult)
-        nc.vector.tensor_scalar(out=wgt_step[:], in0=wgt_sb[:], scalar1=-Z_COEF * STEP, scalar2=None, op0=ALU.mult)
+        nc.gpsimd.tensor_scalar(out=wgt_smooth[:], in0=wgt_sb[:], scalar1=SMOOTH, scalar2=0.0, op0=ALU.mult, op1=ALU.add)
 
         h_bf, h_codes, h_scales = {}, {}, {}
         stats = {}
@@ -100,10 +102,9 @@ def tile_picked_yzloss_grad_p_kernel(tc, x_words, x_scales, hT, goal, wgt, offs,
             nc.vector.tensor_copy(out=picked_planes[:], in_=planes[:].indirect(offsets[:]))
 
         def cast(g, i, copy):
-            h_bf[g, i] = keep.tile([P, P, PACK], BF16, name="h_bf%d%d" % (g, i), align_bytes=64)
-            cols = slice((i % 2) * P, (i % 2 + 1) * P)
+            h_bf[g, i] = keep.tile([P, P, PACK], BF16, name="h_bf%d%d" % (g, i), tag="h_bf%d%d" % (g, i), align_bytes=64)
             copy(out=h_bf[g, i][:].rearrange("p (c e) j -> p c j e", e=4),
-                 in_=h_raw[g, i // 2][:, :, cols].rearrange("p j (c e) -> p c j e", e=4))
+                 in_=h_raw[g, i][:].rearrange("p j (c e) -> p c j e", e=4))
 
         def quantize(g, i):
             h_codes[g, i] = keep.tile([P, P], U32, name="h_codes%d%d" % (g, i), align_bytes=64)
@@ -121,7 +122,11 @@ def tile_picked_yzloss_grad_p_kernel(tc, x_words, x_scales, hT, goal, wgt, offs,
             return stats[name, i][:]
 
         def row_max(i):
-            nc.vector.tensor_reduce(out=stat("neg_max", i), in_=logits[i][:], axis=mybir.AxisListType.X, op=ALU.max, negate=True)
+            if i + 2 < TILES:
+                stats["neg_max", i] = keep.tile([P, 1], F32, name="neg_max%d" % i, tag="h_bf1%d" % (i + 2), align_bytes=64)
+            else:
+                stat("neg_max", i)
+            nc.vector.tensor_reduce(out=stats["neg_max", i][:], in_=logits[i][:], axis=mybir.AxisListType.X, op=ALU.max, negate=True)
 
         expd = [keep.tile([P, S], F32, name="expd%d" % i, align_bytes=64) for i in range(TILES)]
         target = [keep.tile([P, S], F32, name="target%d" % i, align_bytes=64) for i in range(TILES)]
@@ -131,19 +136,19 @@ def tile_picked_yzloss_grad_p_kernel(tc, x_words, x_scales, hT, goal, wgt, offs,
         def exponentiate(i):
             nc.scalar.activation(out=expd[i][:], in_=logits[i][:], func=ACT.Exp, bias=stats["neg_max", i][:], scale=1.0,
                                  accum_out=stat("total", i))
-            nc.scalar.activation(out=decays[i][:], in_=neg_rates[:], func=ACT.Exp, scale=stats["total", i][:],
-                                 accum_out=stat("decay_sum", i))
+            nc.scalar.activation(out=decays[i][:], in_=neg_rates[:], func=ACT.Exp, scale=stats["total", i][:])
+
+        node_weights = [keep.tile([P, NODES], F32, name="node_weights%d" % i) for i in range(TILES)]
+        terms = [keep.tile([P, NODES], F32, name="terms%d" % i) for i in range(TILES)]
 
         def shift(i):
-            nc.vector.tensor_scalar(out=stat("shift", i), in0=stats["neg_max", i][:], scalar1=1.0 / STEP,
-                                    scalar2=-(1.0 + Z_COEF * LOG_CONST) / (Z_COEF * STEP), op0=ALU.mult, op1=ALU.add)
+            nc.vector.scalar_tensor_tensor(out=node_weights[i][:], in0=per_max[:], scalar=stats["neg_max", i][:],
+                                           in1=base[:], op0=ALU.mult, op1=ALU.add)
 
         def factor(i):
-            nc.vector.reciprocal(out=stat("inv_total", i), in_=stats["total", i][:])
-            nc.vector.tensor_scalar(out=stat("gain", i), in0=stats["inv_total", i][:], scalar1=wgt_step[:, i:i + 1],
-                                    scalar2=None, op0=ALU.mult)
-            nc.vector.tensor_scalar(out=stat("factor", i), in0=stats["decay_sum", i][:], scalar1=stats["shift", i][:],
-                                    scalar2=stats["gain", i][:], op0=ALU.add, op1=ALU.mult)
+            nc.vector.scalar_tensor_tensor(out=terms[i][:], in0=decays[i][:], scalar=wgt_sb[:, i:i + 1],
+                                           in1=node_weights[i][:], op0=ALU.mult, op1=ALU.mult,
+                                           accum_out=stat("factor", i))
 
         def weigh_goal(i, eng):
             if eng == "s":
@@ -154,30 +159,31 @@ def tile_picked_yzloss_grad_p_kernel(tc, x_words, x_scales, hT, goal, wgt, offs,
                     out=target[i][:], in0=goal_sb[i][:], scalar1=wgt_sb[:, i:i + 1],
                     scalar2=wgt_smooth[:, i:i + 1], op0=ALU.mult, op1=ALU.add)
 
-        def finish(i):
-            nc.vector.scalar_tensor_tensor(out=result[i][:], in0=expd[i][:], scalar=stats["factor", i][:],
-                                           in1=target[i][:], op0=ALU.mult, op1=ALU.subtract)
-            nc.sync.dma_start(out=out[i * P:(i + 1) * P, :], in_=result[i][:])
+        def finish(i, pieces):
+            width = S // pieces
+            for n in range(pieces):
+                cols = slice(n * width, (n + 1) * width)
+                nc.vector.scalar_tensor_tensor(out=result[i][:, cols], in0=expd[i][:, cols], scalar=stats["factor", i][:],
+                                               in1=target[i][:, cols], op0=ALU.mult, op1=ALU.subtract)
+                nc.sync.dma_start(out=out[i * P:(i + 1) * P, cols], in_=result[i][:, cols])
 
         on_v, on_s = nc.vector.tensor_copy, nc.scalar.copy
         gather_planes()
         for g in range(PASSES):
             gather_words(g)
-        for u in range(2):
+        for i in range(TILES):
             for g in range(PASSES):
-                for i in (2 * u, 2 * u + 1):
-                    cast(g, i, on_s if (i % 2 == 1 or (g, u) == (0, 0)) else on_v)
-                for i in (2 * u, 2 * u + 1):
-                    quantize(g, i)
-                    multiply(g, i)
+                cast(g, i, on_v if g == 1 and i < 2 else on_s)
+            for g in range(PASSES):
+                quantize(g, i)
+                multiply(g, i)
         for i in range(TILES):
             weigh_goal(i, "g")
         for i in range(TILES):
             row_max(i)
             exponentiate(i)
             shift(i)
-            if i > 0:
-                factor(i - 1)
-        factor(TILES - 1)
+            factor(i)
         for i in range(TILES):
-            finish(i)
+            pass
+            finish(i, 2 if i == TILES - 1 else 1)

@@ -1,6 +1,7 @@
 from contextlib import ExitStack
 
 import concourse.mybir as mybir
+from concourse.masks import make_identity
 
 K, T, S, V = 1024, 2048, 512, 512
 FLOPS = 2 * K * S * V
@@ -41,8 +42,7 @@ def tile_picked_yzloss_grad_p_kernel(tc, x_words, x_scales, hT, goal, wgt, offs,
         planes = keep.tile([P, T], U8, name="planes", align_bytes=64)
         picked_words = [keep.tile([P, S], U32, name="picked_words%d" % g, align_bytes=64) for g in range(PASSES)]
         picked_planes = keep.tile([P, S], U8, name="picked_planes", align_bytes=64)
-        h_raw = {(g, u): keep.tile([P, PACK, P], F32, name="h_raw%d%d" % (g, u), align_bytes=64)
-                 for g in range(PASSES) for u in range(TILES)}
+        h_raw = {}
         goal_sb = [keep.tile([P, S], F32, name="goal%d" % i, align_bytes=64) for i in range(TILES)]
         wgt_sb = keep.tile([P, TILES], F32, name="wgt_sb")
         logits = [psum.tile([P, S], F32, name="logits%d" % i) for i in range(TILES)]
@@ -50,9 +50,12 @@ def tile_picked_yzloss_grad_p_kernel(tc, x_words, x_scales, hT, goal, wgt, offs,
         def load_words(g):
             nc.sync.dma_start(out=words[g][:].bitcast(I32), in_=x_words[g].rearrange("p n t -> p (n t)").bitcast(I32))
 
-        def load_h(g, u):
-            rows = hT[g * K_PASS:(g + 1) * K_PASS, u * P:(u + 1) * P]
-            nc.sync.dma_start(out=h_raw[g, u][:], in_=rows.rearrange("(p j) w -> p j w", j=PACK))
+        def load_h(g, first, count):
+            raw = keep.tile([P, PACK, count * P], F32, name="h_raw%d%d" % (g, first), align_bytes=64)
+            rows = hT[g * K_PASS:(g + 1) * K_PASS, first * P:(first + count) * P]
+            nc.sync.dma_start(out=raw[:], in_=rows.rearrange("(p j) w -> p j w", j=PACK))
+            for n in range(count):
+                h_raw[g, first + n] = raw[:, :, n * P:(n + 1) * P]
 
         def load_planes():
             for q in range(4):
@@ -67,12 +70,10 @@ def tile_picked_yzloss_grad_p_kernel(tc, x_words, x_scales, hT, goal, wgt, offs,
         nc.sync.dma_start(offsets[:], offs)
         load_words(0)
         load_planes()
+        load_h(0, 0, TILES)
         load_words(1)
-        for i in range(TILES):
-            for g in range(PASSES):
-                load_h(g, i)
-        with nc.allow_non_contiguous_dma(reason="one weight a partition"):
-            nc.sync.dma_start(out=wgt_sb[:], in_=wgt.rearrange("(i p) o -> p (i o)", p=P))
+        load_h(1, 0, 2)
+        load_h(1, 2, 2)
         for i in range(TILES):
             load_goal(i)
 
@@ -89,8 +90,16 @@ def tile_picked_yzloss_grad_p_kernel(tc, x_words, x_scales, hT, goal, wgt, offs,
                                 scalar2=STEP * (1.0 - Z_COEF * (EULER + FIRST)), op0=ALU.mult, op1=ALU.add)
         base = keep.tile([P, NODES], F32, name="base")
         nc.vector.tensor_tensor(out=base[:], in0=log_term[:], in1=rates[:], op=ALU.mult)
+        identity = keep.tile([P, P], F32, name="identity")
+        make_identity(nc, identity[:])
+        wgt_rows = keep.tile([P, P], F32, name="wgt_rows")
+        nc.vector.memset(wgt_rows[:], 0.0)
+        nc.scalar.dma_start(out=wgt_rows[:TILES, :], in_=wgt.rearrange("(i p) o -> i (p o)", p=P))
+        wgt_turned = psum.tile([P, P], F32, name="wgt_turned")
+        nc.tensor.transpose(wgt_turned[:], wgt_rows[:], identity[:])
+        nc.vector.tensor_copy(out=wgt_sb[:], in_=wgt_turned[:, :TILES])
         wgt_smooth = keep.tile([P, TILES], F32, name="wgt_smooth")
-        nc.gpsimd.tensor_scalar(out=wgt_smooth[:], in0=wgt_sb[:], scalar1=SMOOTH, scalar2=0.0, op0=ALU.mult, op1=ALU.add)
+        nc.vector.tensor_scalar(out=wgt_smooth[:], in0=wgt_sb[:], scalar1=SMOOTH, scalar2=0.0, op0=ALU.mult, op1=ALU.add)
 
         h_bf, h_codes, h_scales = {}, {}, {}
         stats = {}
@@ -104,7 +113,7 @@ def tile_picked_yzloss_grad_p_kernel(tc, x_words, x_scales, hT, goal, wgt, offs,
         def cast(g, i, copy):
             h_bf[g, i] = keep.tile([P, P, PACK], BF16, name="h_bf%d%d" % (g, i), tag="h_bf%d%d" % (g, i), align_bytes=64)
             copy(out=h_bf[g, i][:].rearrange("p (c e) j -> p c j e", e=4),
-                 in_=h_raw[g, i][:].rearrange("p j (c e) -> p c j e", e=4))
+                 in_=h_raw[g, i].rearrange("p j (c e) -> p c j e", e=4))
 
         def quantize(g, i):
             h_codes[g, i] = keep.tile([P, P], U32, name="h_codes%d%d" % (g, i), align_bytes=64)
@@ -171,19 +180,18 @@ def tile_picked_yzloss_grad_p_kernel(tc, x_words, x_scales, hT, goal, wgt, offs,
         gather_planes()
         for g in range(PASSES):
             gather_words(g)
-        for i in range(TILES):
-            for g in range(PASSES):
-                cast(g, i, on_v if g == 1 and i < 2 else on_s)
-            for g in range(PASSES):
-                quantize(g, i)
-                multiply(g, i)
-        for i in range(TILES):
-            weigh_goal(i, "g")
+        for g in range(PASSES):
+            for pair in range(0, TILES, 2):
+                for i in (pair, pair + 1):
+                    cast(g, i, on_v if i % 2 else on_s)
+                for i in (pair, pair + 1):
+                    quantize(g, i)
+                    multiply(g, i)
         for i in range(TILES):
             row_max(i)
             exponentiate(i)
             shift(i)
             factor(i)
         for i in range(TILES):
-            pass
+            weigh_goal(i, "s")
             finish(i, 2 if i == TILES - 1 else 1)

@@ -21,13 +21,18 @@ PACK = 4
 K_PASS = P * PACK
 PASSES = K // K_PASS
 TILES = V // P
+PAIR = 2
+QUADRANTS = 4
+SCALE_ROWS = 4
+RUN = 4
 
 Z_COEF = 0.2
 SMOOTH = 0.0002
 
-NODES = 84
-STEP = 0.4
-FIRST = -30.0
+NODES = 36
+STEP = 0.34
+FIRST = -3.25
+LOG_SCALE = -5.5
 EULER = 0.5772156649015329
 
 
@@ -58,140 +63,115 @@ def tile_picked_yzloss_grad_p_kernel(tc, x_words, x_scales, hT, goal, wgt, offs,
                 h_raw[g, first + n] = raw[:, :, n * P:(n + 1) * P]
 
         def load_planes():
-            for q in range(4):
-                nc.sync.dma_start(out=planes[32 * q:32 * q + 4 * PASSES, :].bitcast(I32),
-                                  in_=x_scales[:, 4 * q:4 * q + 4, :].bitcast(I32))
-
-        def load_goal(i):
-            nc.sync.dma_start(out=goal_sb[i][:], in_=goal[i * P:(i + 1) * P, :])
+            for q in range(QUADRANTS):
+                step = PASSES if q < QUADRANTS // 2 else 1
+                for g in range(0, PASSES, step):
+                    nc.sync.dma_start(
+                        out=planes[32 * q + SCALE_ROWS * g:32 * q + SCALE_ROWS * (g + step), :].bitcast(I32),
+                        in_=x_scales[g:g + step, SCALE_ROWS * q:SCALE_ROWS * (q + 1), :].bitcast(I32))
 
         nc.vector.memset(planes[:, :T // 2].bitcast(I32), 0)
         nc.gpsimd.memset(planes[:, T // 2:].bitcast(I32), 0)
+        wgt_rows = keep.tile([P, P], F32, name="wgt_rows")
+        nc.vector.memset(wgt_rows[:], 0.0)
+
         nc.sync.dma_start(offsets[:], offs)
         load_words(0)
         load_planes()
         load_h(0, 0, TILES)
+        nc.sync.dma_start(out=wgt_rows[:TILES, :], in_=wgt.rearrange("(i p) o -> i (p o)", p=P))
         load_words(1)
-        load_h(1, 0, 2)
-        load_h(1, 2, 2)
+        for first in range(0, TILES, PAIR):
+            load_h(1, first, PAIR)
         for i in range(TILES):
-            load_goal(i)
+            nc.sync.dma_start(out=goal_sb[i][:], in_=goal[i * P:(i + 1) * P, :])
 
         index = keep.tile([P, NODES], F32, name="index")
         nc.gpsimd.iota(index[:], [[1, NODES]], base=0, channel_multiplier=0, allow_small_or_imprecise_dtypes=True)
-        rates = keep.tile([P, NODES], F32, name="rates")
-        nc.scalar.activation(out=rates[:], in_=index[:], func=ACT.Exp, scale=STEP, bias=FIRST)
-        neg_rates = keep.tile([P, NODES], F32, name="neg_rates")
+        bend, u_shifted, log_rates, rates, neg_rates, slope, per_max, log_term, base = (
+            keep.tile([P, NODES], F32, name=name)
+            for name in ("bend", "u_shifted", "log_rates", "rates", "neg_rates", "slope", "per_max", "log_term", "base"))
+        nc.scalar.activation(out=bend[:], in_=index[:], func=ACT.Exp, scale=-STEP, bias=-FIRST)
+        nc.vector.tensor_scalar(out=u_shifted[:], in0=index[:], scalar1=STEP, scalar2=FIRST + LOG_SCALE,
+                                op0=ALU.mult, op1=ALU.add)
+        nc.vector.tensor_tensor(out=log_rates[:], in0=u_shifted[:], in1=bend[:], op=ALU.subtract)
+        nc.scalar.activation(out=rates[:], in_=log_rates[:], func=ACT.Exp)
         nc.vector.tensor_scalar(out=neg_rates[:], in0=rates[:], scalar1=-1.0, scalar2=None, op0=ALU.mult)
-        per_max = keep.tile([P, NODES], F32, name="per_max")
-        nc.vector.tensor_scalar(out=per_max[:], in0=rates[:], scalar1=-Z_COEF * STEP, scalar2=None, op0=ALU.mult)
-        log_term = keep.tile([P, NODES], F32, name="log_term")
-        nc.vector.tensor_scalar(out=log_term[:], in0=index[:], scalar1=-Z_COEF * STEP * STEP,
-                                scalar2=STEP * (1.0 - Z_COEF * (EULER + FIRST)), op0=ALU.mult, op1=ALU.add)
-        base = keep.tile([P, NODES], F32, name="base")
-        nc.vector.tensor_tensor(out=base[:], in0=log_term[:], in1=rates[:], op=ALU.mult)
+        nc.vector.scalar_tensor_tensor(out=slope[:], in0=bend[:], scalar=1.0, in1=rates[:], op0=ALU.add, op1=ALU.mult)
+        nc.vector.tensor_scalar(out=per_max[:], in0=slope[:], scalar1=-Z_COEF * STEP, scalar2=None, op0=ALU.mult)
+        nc.vector.tensor_scalar(out=log_term[:], in0=log_rates[:], scalar1=-Z_COEF * STEP,
+                                scalar2=STEP * (1.0 - Z_COEF * EULER), op0=ALU.mult, op1=ALU.add)
+        nc.vector.tensor_tensor(out=base[:], in0=log_term[:], in1=slope[:], op=ALU.mult)
+
         identity = keep.tile([P, P], F32, name="identity")
         make_identity(nc, identity[:])
-        wgt_rows = keep.tile([P, P], F32, name="wgt_rows")
-        nc.vector.memset(wgt_rows[:], 0.0)
-        nc.scalar.dma_start(out=wgt_rows[:TILES, :], in_=wgt.rearrange("(i p) o -> i (p o)", p=P))
         wgt_turned = psum.tile([P, P], F32, name="wgt_turned")
         nc.tensor.transpose(wgt_turned[:], wgt_rows[:], identity[:])
         nc.vector.tensor_copy(out=wgt_sb[:], in_=wgt_turned[:, :TILES])
         wgt_smooth = keep.tile([P, TILES], F32, name="wgt_smooth")
         nc.vector.tensor_scalar(out=wgt_smooth[:], in0=wgt_sb[:], scalar1=SMOOTH, scalar2=0.0, op0=ALU.mult, op1=ALU.add)
 
-        h_bf, h_codes, h_scales = {}, {}, {}
-        stats = {}
-
-        def gather_words(g):
-            nc.vector.tensor_copy(out=picked_words[g][:], in_=words[g][:].indirect(offsets[:]))
-
-        def gather_planes():
-            nc.vector.tensor_copy(out=picked_planes[:], in_=planes[:].indirect(offsets[:]))
-
-        def cast(g, i, copy):
-            h_bf[g, i] = keep.tile([P, P, PACK], BF16, name="h_bf%d%d" % (g, i), tag="h_bf%d%d" % (g, i), align_bytes=64)
-            copy(out=h_bf[g, i][:].rearrange("p (c e) j -> p c j e", e=4),
-                 in_=h_raw[g, i].rearrange("p j (c e) -> p c j e", e=4))
-
-        def quantize(g, i):
-            h_codes[g, i] = keep.tile([P, P], U32, name="h_codes%d%d" % (g, i), align_bytes=64)
-            h_scales[g, i] = keep.tile([P, P], U8, name="h_scales%d%d" % (g, i), align_bytes=64)
-            nc.vector.quantize_mx(out=h_codes[g, i][:].bitcast(FP8X4), scales=h_scales[g, i][:],
-                                  in_=h_bf[g, i][:].rearrange("p c j -> p (c j)"))
-
-        def multiply(g, i):
-            nc.tensor.matmul_mx(out=logits[i][:], lhsT=h_codes[g, i][:].bitcast(FP8X4), lhsT_scale=h_scales[g, i][:],
-                                rhs=picked_words[g][:].bitcast(FP8X4), rhs_scale=picked_planes[4 * g:, :],
-                                start=(g == 0), stop=(g == PASSES - 1))
-
-        def stat(name, i):
-            stats[name, i] = keep.tile([P, 1], F32, name="%s%d" % (name, i))
-            return stats[name, i][:]
-
-        def row_max(i):
-            if i + 2 < TILES:
-                stats["neg_max", i] = keep.tile([P, 1], F32, name="neg_max%d" % i, tag="h_bf1%d" % (i + 2), align_bytes=64)
-            else:
-                stat("neg_max", i)
-            nc.vector.tensor_reduce(out=stats["neg_max", i][:], in_=logits[i][:], axis=mybir.AxisListType.X, op=ALU.max, negate=True)
-
         expd = [keep.tile([P, S], F32, name="expd%d" % i, align_bytes=64) for i in range(TILES)]
         target = [keep.tile([P, S], F32, name="target%d" % i, align_bytes=64) for i in range(TILES)]
         result = [keep.tile([P, S], F32, name="result%d" % i, align_bytes=64) for i in range(TILES)]
         decays = [keep.tile([P, NODES], F32, name="decays%d" % i) for i in range(TILES)]
-
-        def exponentiate(i):
-            nc.scalar.activation(out=expd[i][:], in_=logits[i][:], func=ACT.Exp, bias=stats["neg_max", i][:], scale=1.0,
-                                 accum_out=stat("total", i))
-            nc.scalar.activation(out=decays[i][:], in_=neg_rates[:], func=ACT.Exp, scale=stats["total", i][:])
-
         node_weights = [keep.tile([P, NODES], F32, name="node_weights%d" % i) for i in range(TILES)]
         terms = [keep.tile([P, NODES], F32, name="terms%d" % i) for i in range(TILES)]
+        h_bf, factors = {}, []
 
-        def shift(i):
-            nc.vector.scalar_tensor_tensor(out=node_weights[i][:], in0=per_max[:], scalar=stats["neg_max", i][:],
-                                           in1=base[:], op0=ALU.mult, op1=ALU.add)
+        def cast(g, i):
+            h_bf[g, i] = keep.tile([P, P, PACK], BF16, name="h_bf%d%d" % (g, i), tag="h_bf%d%d" % (g, i), align_bytes=64)
+            copy = nc.vector.tensor_copy if i % 2 else nc.scalar.copy
+            copy(out=h_bf[g, i][:].rearrange("p (c e) j -> p c j e", e=RUN),
+                 in_=h_raw[g, i].rearrange("p j (c e) -> p c j e", e=RUN))
 
-        def factor(i):
-            nc.vector.scalar_tensor_tensor(out=terms[i][:], in0=decays[i][:], scalar=wgt_sb[:, i:i + 1],
-                                           in1=node_weights[i][:], op0=ALU.mult, op1=ALU.mult,
-                                           accum_out=stat("factor", i))
+        def quantize_and_multiply(g, i):
+            codes = keep.tile([P, P], U32, name="h_codes%d%d" % (g, i), align_bytes=64)
+            scales = keep.tile([P, P], U8, name="h_scales%d%d" % (g, i), align_bytes=64)
+            nc.vector.quantize_mx(out=codes[:].bitcast(FP8X4), scales=scales[:],
+                                  in_=h_bf[g, i][:].rearrange("p c j -> p (c j)"))
+            nc.tensor.matmul_mx(out=logits[i][:], lhsT=codes[:].bitcast(FP8X4), lhsT_scale=scales[:],
+                                rhs=picked_words[g][:].bitcast(FP8X4), rhs_scale=picked_planes[SCALE_ROWS * g:, :],
+                                start=(g == 0), stop=(g == PASSES - 1))
 
-        def weigh_goal(i, eng):
-            if eng == "s":
-                nc.scalar.activation(out=target[i][:], in_=goal_sb[i][:], func=ACT.Identity,
-                                     scale=wgt_sb[:, i:i + 1], bias=wgt_smooth[:, i:i + 1])
+        def softmax_and_factor(i):
+            if i == PAIR - 1:
+                neg_max = keep.tile([P, 1], F32, name="neg_max%d" % i, tag="h_bf%d%d" % (PASSES - 1, TILES - 1),
+                                    align_bytes=64)
             else:
-                (nc.vector if eng == "v" else nc.gpsimd).tensor_scalar(
-                    out=target[i][:], in0=goal_sb[i][:], scalar1=wgt_sb[:, i:i + 1],
-                    scalar2=wgt_smooth[:, i:i + 1], op0=ALU.mult, op1=ALU.add)
+                neg_max = keep.tile([P, 1], F32, name="neg_max%d" % i)
+            nc.vector.tensor_reduce(out=neg_max[:], in_=logits[i][:], axis=mybir.AxisListType.X, op=ALU.max, negate=True)
+            total = keep.tile([P, 1], F32, name="total%d" % i)
+            nc.scalar.activation(out=expd[i][:], in_=logits[i][:], func=ACT.Exp, bias=neg_max[:], scale=1.0,
+                                 accum_out=total[:])
+            nc.scalar.activation(out=decays[i][:], in_=neg_rates[:], func=ACT.Exp, scale=total[:])
+            nc.vector.scalar_tensor_tensor(out=node_weights[i][:], in0=per_max[:], scalar=neg_max[:], in1=base[:],
+                                           op0=ALU.mult, op1=ALU.add)
+            factor = keep.tile([P, 1], F32, name="factor%d" % i)
+            nc.vector.scalar_tensor_tensor(out=terms[i][:], in0=decays[i][:], scalar=wgt_sb[:, i:i + 1],
+                                           in1=node_weights[i][:], op0=ALU.mult, op1=ALU.mult, accum_out=factor[:])
+            factors.append(factor)
 
-        def finish(i, pieces):
-            width = S // pieces
-            for n in range(pieces):
-                cols = slice(n * width, (n + 1) * width)
-                nc.vector.scalar_tensor_tensor(out=result[i][:, cols], in0=expd[i][:, cols], scalar=stats["factor", i][:],
+        def finish(i):
+            nc.scalar.activation(out=target[i][:], in_=goal_sb[i][:], func=ACT.Identity,
+                                 scale=wgt_sb[:, i:i + 1], bias=wgt_smooth[:, i:i + 1])
+            width = S // 2 if i == TILES - 1 else S
+            for col in range(0, S, width):
+                cols = slice(col, col + width)
+                nc.vector.scalar_tensor_tensor(out=result[i][:, cols], in0=expd[i][:, cols], scalar=factors[i][:],
                                                in1=target[i][:, cols], op0=ALU.mult, op1=ALU.subtract)
                 nc.sync.dma_start(out=out[i * P:(i + 1) * P, cols], in_=result[i][:, cols])
 
-        on_v, on_s = nc.vector.tensor_copy, nc.scalar.copy
-        gather_planes()
+        nc.vector.tensor_copy(out=picked_planes[:], in_=planes[:].indirect(offsets[:]))
         for g in range(PASSES):
-            gather_words(g)
+            nc.vector.tensor_copy(out=picked_words[g][:], in_=words[g][:].indirect(offsets[:]))
         for g in range(PASSES):
-            for pair in range(0, TILES, 2):
-                for i in (pair, pair + 1):
-                    cast(g, i, on_v if i % 2 else on_s)
-                for i in (pair, pair + 1):
-                    quantize(g, i)
-                    multiply(g, i)
+            for first in range(0, TILES, PAIR):
+                for i in range(first, first + PAIR):
+                    cast(g, i)
+                for i in range(first, first + PAIR):
+                    quantize_and_multiply(g, i)
         for i in range(TILES):
-            row_max(i)
-            exponentiate(i)
-            shift(i)
-            factor(i)
+            softmax_and_factor(i)
         for i in range(TILES):
-            weigh_goal(i, "s")
-            finish(i, 2 if i == TILES - 1 else 1)
+            finish(i)

from contextlib import ExitStack

import concourse.mybir as mybir
from concourse.masks import make_identity

K, T, S, V = 1024, 2048, 512, 512
FLOPS = 2 * K * S * V

F32 = mybir.dt.float32
BF16 = mybir.dt.bfloat16
I32 = mybir.dt.int32
U32 = mybir.dt.uint32
U16 = mybir.dt.uint16
U8 = mybir.dt.uint8
FP8X4 = mybir.dt.float8_e4m3fn_x4
ALU = mybir.AluOpType
ACT = mybir.ActivationFunctionType

P = 128
PACK = 4
K_PASS = P * PACK
PASSES = K // K_PASS
TILES = V // P
PAIR = 2
QUADRANTS = 4
SCALE_ROWS = 4
RUN = 4

Z_COEF = 0.2
SMOOTH = 0.0002

NODES = 36
STEP = 0.34
FIRST = -3.25
LOG_SCALE = -5.5
EULER = 0.5772156649015329


def tile_picked_yzloss_grad_p_kernel(tc, x_words, x_scales, hT, goal, wgt, offs, out):
    nc = tc.nc
    with ExitStack() as ctx:
        keep = ctx.enter_context(tc.tile_pool(name="keep", bufs=1))
        psum = ctx.enter_context(tc.psum_pool(name="psum", bufs=1))

        offsets = keep.tile([P, S // 16], U16, name="offsets")
        words = [keep.tile([P, T], U32, name="words%d" % g, align_bytes=64) for g in range(PASSES)]
        planes = keep.tile([P, T], U8, name="planes", align_bytes=64)
        picked_words = [keep.tile([P, S], U32, name="picked_words%d" % g, align_bytes=64) for g in range(PASSES)]
        picked_planes = keep.tile([P, S], U8, name="picked_planes", align_bytes=64)
        h_raw = {}
        goal_sb = [keep.tile([P, S], F32, name="goal%d" % i, align_bytes=64) for i in range(TILES)]
        wgt_sb = keep.tile([P, TILES], F32, name="wgt_sb")
        logits = [psum.tile([P, S], F32, name="logits%d" % i) for i in range(TILES)]

        def load_words(g):
            nc.sync.dma_start(out=words[g][:].bitcast(I32), in_=x_words[g].rearrange("p n t -> p (n t)").bitcast(I32))

        def load_h(g, first, count):
            raw = keep.tile([P, PACK, count * P], F32, name="h_raw%d%d" % (g, first), align_bytes=64)
            rows = hT[g * K_PASS:(g + 1) * K_PASS, first * P:(first + count) * P]
            nc.sync.dma_start(out=raw[:], in_=rows.rearrange("(p j) w -> p j w", j=PACK))
            for n in range(count):
                h_raw[g, first + n] = raw[:, :, n * P:(n + 1) * P]

        def load_planes():
            for q in range(QUADRANTS):
                step = PASSES if q < QUADRANTS // 2 else 1
                for g in range(0, PASSES, step):
                    nc.sync.dma_start(
                        out=planes[32 * q + SCALE_ROWS * g:32 * q + SCALE_ROWS * (g + step), :].bitcast(I32),
                        in_=x_scales[g:g + step, SCALE_ROWS * q:SCALE_ROWS * (q + 1), :].bitcast(I32))

        nc.vector.memset(planes[:, :T // 2].bitcast(I32), 0)
        nc.gpsimd.memset(planes[:, T // 2:].bitcast(I32), 0)
        wgt_rows = keep.tile([P, P], F32, name="wgt_rows")
        nc.vector.memset(wgt_rows[:], 0.0)

        nc.sync.dma_start(offsets[:], offs)
        load_words(0)
        load_planes()
        load_h(0, 0, TILES)
        nc.sync.dma_start(out=wgt_rows[:TILES, :], in_=wgt.rearrange("(i p) o -> i (p o)", p=P))
        load_words(1)
        for first in range(0, TILES, PAIR):
            load_h(1, first, PAIR)
        for i in range(TILES):
            nc.sync.dma_start(out=goal_sb[i][:], in_=goal[i * P:(i + 1) * P, :])

        index = keep.tile([P, NODES], F32, name="index")
        nc.gpsimd.iota(index[:], [[1, NODES]], base=0, channel_multiplier=0, allow_small_or_imprecise_dtypes=True)
        bend, u_shifted, log_rates, rates, neg_rates, slope, per_max, log_term, base = (
            keep.tile([P, NODES], F32, name=name)
            for name in ("bend", "u_shifted", "log_rates", "rates", "neg_rates", "slope", "per_max", "log_term", "base"))
        nc.scalar.activation(out=bend[:], in_=index[:], func=ACT.Exp, scale=-STEP, bias=-FIRST)
        nc.vector.tensor_scalar(out=u_shifted[:], in0=index[:], scalar1=STEP, scalar2=FIRST + LOG_SCALE,
                                op0=ALU.mult, op1=ALU.add)
        nc.vector.tensor_tensor(out=log_rates[:], in0=u_shifted[:], in1=bend[:], op=ALU.subtract)
        nc.scalar.activation(out=rates[:], in_=log_rates[:], func=ACT.Exp)
        nc.vector.tensor_scalar(out=neg_rates[:], in0=rates[:], scalar1=-1.0, scalar2=None, op0=ALU.mult)
        nc.vector.scalar_tensor_tensor(out=slope[:], in0=bend[:], scalar=1.0, in1=rates[:], op0=ALU.add, op1=ALU.mult)
        nc.vector.tensor_scalar(out=per_max[:], in0=slope[:], scalar1=-Z_COEF * STEP, scalar2=None, op0=ALU.mult)
        nc.vector.tensor_scalar(out=log_term[:], in0=log_rates[:], scalar1=-Z_COEF * STEP,
                                scalar2=STEP * (1.0 - Z_COEF * EULER), op0=ALU.mult, op1=ALU.add)
        nc.vector.tensor_tensor(out=base[:], in0=log_term[:], in1=slope[:], op=ALU.mult)

        identity = keep.tile([P, P], F32, name="identity")
        make_identity(nc, identity[:])
        wgt_turned = psum.tile([P, P], F32, name="wgt_turned")
        nc.tensor.transpose(wgt_turned[:], wgt_rows[:], identity[:])
        nc.vector.tensor_copy(out=wgt_sb[:], in_=wgt_turned[:, :TILES])
        wgt_smooth = keep.tile([P, TILES], F32, name="wgt_smooth")
        nc.vector.tensor_scalar(out=wgt_smooth[:], in0=wgt_sb[:], scalar1=SMOOTH, scalar2=0.0, op0=ALU.mult, op1=ALU.add)

        expd = [keep.tile([P, S], F32, name="expd%d" % i, align_bytes=64) for i in range(TILES)]
        target = [keep.tile([P, S], F32, name="target%d" % i, align_bytes=64) for i in range(TILES)]
        result = [keep.tile([P, S], F32, name="result%d" % i, align_bytes=64) for i in range(TILES)]
        decays = [keep.tile([P, NODES], F32, name="decays%d" % i) for i in range(TILES)]
        node_weights = [keep.tile([P, NODES], F32, name="node_weights%d" % i) for i in range(TILES)]
        terms = [keep.tile([P, NODES], F32, name="terms%d" % i) for i in range(TILES)]
        h_bf, factors = {}, []

        def cast(g, i):
            h_bf[g, i] = keep.tile([P, P, PACK], BF16, name="h_bf%d%d" % (g, i), tag="h_bf%d%d" % (g, i), align_bytes=64)
            copy = nc.vector.tensor_copy if i % 2 else nc.scalar.copy
            copy(out=h_bf[g, i][:].rearrange("p (c e) j -> p c j e", e=RUN),
                 in_=h_raw[g, i].rearrange("p j (c e) -> p c j e", e=RUN))

        def quantize_and_multiply(g, i):
            codes = keep.tile([P, P], U32, name="h_codes%d%d" % (g, i), align_bytes=64)
            scales = keep.tile([P, P], U8, name="h_scales%d%d" % (g, i), align_bytes=64)
            nc.vector.quantize_mx(out=codes[:].bitcast(FP8X4), scales=scales[:],
                                  in_=h_bf[g, i][:].rearrange("p c j -> p (c j)"))
            nc.tensor.matmul_mx(out=logits[i][:], lhsT=codes[:].bitcast(FP8X4), lhsT_scale=scales[:],
                                rhs=picked_words[g][:].bitcast(FP8X4), rhs_scale=picked_planes[SCALE_ROWS * g:, :],
                                start=(g == 0), stop=(g == PASSES - 1))

        def softmax_and_factor(i):
            if i == PAIR - 1:
                neg_max = keep.tile([P, 1], F32, name="neg_max%d" % i, tag="h_bf%d%d" % (PASSES - 1, TILES - 1),
                                    align_bytes=64)
            else:
                neg_max = keep.tile([P, 1], F32, name="neg_max%d" % i)
            nc.vector.tensor_reduce(out=neg_max[:], in_=logits[i][:], axis=mybir.AxisListType.X, op=ALU.max, negate=True)
            total = keep.tile([P, 1], F32, name="total%d" % i)
            nc.scalar.activation(out=expd[i][:], in_=logits[i][:], func=ACT.Exp, bias=neg_max[:], scale=1.0,
                                 accum_out=total[:])
            nc.scalar.activation(out=decays[i][:], in_=neg_rates[:], func=ACT.Exp, scale=total[:])
            nc.vector.scalar_tensor_tensor(out=node_weights[i][:], in0=per_max[:], scalar=neg_max[:], in1=base[:],
                                           op0=ALU.mult, op1=ALU.add)
            factor = keep.tile([P, 1], F32, name="factor%d" % i)
            nc.vector.scalar_tensor_tensor(out=terms[i][:], in0=decays[i][:], scalar=wgt_sb[:, i:i + 1],
                                           in1=node_weights[i][:], op0=ALU.mult, op1=ALU.mult, accum_out=factor[:])
            factors.append(factor)

        def finish(i):
            nc.scalar.activation(out=target[i][:], in_=goal_sb[i][:], func=ACT.Identity,
                                 scale=wgt_sb[:, i:i + 1], bias=wgt_smooth[:, i:i + 1])
            width = S // 2 if i == TILES - 1 else S
            for col in range(0, S, width):
                cols = slice(col, col + width)
                nc.vector.scalar_tensor_tensor(out=result[i][:, cols], in0=expd[i][:, cols], scalar=factors[i][:],
                                               in1=target[i][:, cols], op0=ALU.mult, op1=ALU.subtract)
                nc.sync.dma_start(out=out[i * P:(i + 1) * P, cols], in_=result[i][:, cols])

        nc.vector.tensor_copy(out=picked_planes[:], in_=planes[:].indirect(offsets[:]))
        for g in range(PASSES):
            nc.vector.tensor_copy(out=picked_words[g][:], in_=words[g][:].indirect(offsets[:]))
        for g in range(PASSES):
            for first in range(0, TILES, PAIR):
                for i in range(first, first + PAIR):
                    cast(g, i)
                for i in range(first, first + PAIR):
                    quantize_and_multiply(g, i)
        for i in range(TILES):
            softmax_and_factor(i)
        for i in range(TILES):
            finish(i)
